import numpy as np
import ml_dtypes


def mxq(x, axis, fmt="e4m3"):
    dtype, down = {"e4m3": (ml_dtypes.float8_e4m3fn, 7), "e5m2": (ml_dtypes.float8_e5m2, 14)}[fmt]
    v = np.moveaxis(np.asarray(x, np.float32).astype(ml_dtypes.bfloat16).astype(np.float64), axis, -1)
    blocks = v.reshape(v.shape[:-1] + (-1, 32))
    amax = np.abs(blocks).max(-1, keepdims=True)
    byte = np.maximum(np.where(amax > 0, np.frexp(amax)[1] - 1 + 127, 0) - down, 1)
    scale = np.exp2(byte - 127.0)
    codes = (blocks / scale).astype(np.float32).astype(dtype).astype(np.float64)
    return np.moveaxis((codes * scale).reshape(v.shape), -1, axis)


WIDE = False


def mx_kscale(k):
    if not WIDE:
        return np.ones(k)
    levels = np.array([10, -10, 5, -5, 0])
    if k % 512:
        return np.exp2(np.random.permutation(np.resize(levels, k // 32))).repeat(32)
    a = np.empty((k // 512, 16))
    for p in range(k // 512):
        a[p, :8] = np.random.permutation(np.resize(levels, 8))
        for g in range(8):
            far = levels[np.abs(levels - a[p, g]) >= 10]
            a[p, g + 8] = far[np.random.randint(len(far))]
    return np.exp2(a.ravel()).repeat(32)


def f64(x):
    return np.asarray(x).astype(np.float64)


def striped(idx):
    return np.tile(idx.reshape(-1, 16).T, (8, 1)).astype(np.uint16)


def unstriped(offs):
    return offs[:16].T.reshape(-1).astype(np.int64)


def striped8(idx):
    return np.concatenate([x.reshape(-1, 16).T for x in idx]).astype(np.uint16)


def runs(offs, k):
    lists = np.stack([offs[16 * r : 16 * r + 16].T.reshape(-1) for r in range(8)]).astype(np.int64)
    return lists[np.arange(k) % 512 // 64]


def pack_weight(w):
    k, n = w.shape
    w = f64(np.asarray(w, np.float32).astype(ml_dtypes.bfloat16)).reshape(k // 32, 32, n)
    amax = np.abs(w).max(1)
    byte = np.clip(np.where(amax > 0, np.frexp(amax)[1] - 1 + 127 - 7, 1), 1, 254)
    scaled = (w * np.exp2(127.0 - byte)[:, None, :]).reshape(k, n).astype(np.float32)
    words = np.ascontiguousarray(scaled.reshape(k // 512, 128, 4, n).transpose(0, 1, 3, 2)).astype(ml_dtypes.float8_e4m3fn).view(np.uint8)
    return words, np.ascontiguousarray(byte.astype(np.uint8).reshape(k // 512, 16, n))


def unpack_weight(words, scales):
    g, p, n, _ = words.shape
    vals = np.ascontiguousarray(words).view(ml_dtypes.float8_e4m3fn).astype(np.float64) * np.repeat(np.exp2(scales.astype(np.float64) - 127.0), 8, axis=1)[..., None]
    return vals.transpose(0, 1, 3, 2).reshape(g * 512, n)


E2M1 = np.array([0.0, 0.5, 1.0, 1.5, 2.0, 3.0, 4.0, 6.0, -0.0, -0.5, -1.0, -1.5, -2.0, -3.0, -4.0, -6.0])


def pack_fp4(w):
    k, n = w.shape
    w = f64(np.asarray(w, np.float32).astype(ml_dtypes.bfloat16)).reshape(k // 32, 32, n)
    amax = np.abs(w).max(1)
    mant, ex = np.frexp(amax / 6.0)
    byte = np.clip(np.where(amax > 0, np.where(mant > 0.5, ex, ex - 1) + 127, 1), 1, 254)
    scaled = (w * np.exp2(127.0 - byte)[:, None, :]).reshape(k, n).astype(np.float32)
    c = np.ascontiguousarray(scaled.reshape(k // 512, 128, 4, n).transpose(0, 1, 3, 2)).astype(ml_dtypes.float4_e2m1fn).view(np.uint8) & 0xF
    words = (c[..., 0::2] | (c[..., 1::2] << 4)).reshape(k // 512, 128, 2 * n)
    return np.ascontiguousarray(words), np.ascontiguousarray(byte.astype(np.uint8).reshape(k // 512, 16, n))


def unpack_fp4(words, scales):
    g, _, n = scales.shape
    words = np.ascontiguousarray(words).reshape(g, 128, n, 2)
    nib = np.empty((g, 128, n, 4), np.uint8)
    nib[..., 0::2] = words & 0xF
    nib[..., 1::2] = words >> 4
    vals = E2M1[nib] * np.repeat(np.exp2(scales.astype(np.float64) - 127.0), 8, axis=1)[..., None]
    return vals.transpose(0, 1, 3, 2).reshape(g * 512, n)


def sigmoid(v):
    return 1.0 / (1.0 + np.exp(-np.maximum(v, -700.0)))

def planes(y):
    n, m = y.shape
    v = y.astype(np.float32).astype(ml_dtypes.bfloat16).astype(np.float64).reshape(n // 32, 32, m)
    top = np.abs(v).max(1)
    byte = np.clip(np.where(top > 0, np.frexp(top)[1] - 1 + 127 - 7, 1), 1, 254)
    codes = (v * np.exp2(127.0 - byte)[:, None, :]).reshape(n, m).astype(np.float32).astype(ml_dtypes.float8_e4m3fn).view(np.uint8)
    words = codes.reshape(n // 512, 128, 4, m).transpose(0, 1, 3, 2)
    return np.ascontiguousarray(words), np.ascontiguousarray(byte.astype(np.uint8).reshape(n // 512, 16, m))


K, T, S, N, H, G, W = 512, 1024, 512, 512, 512, 2048, 1024


def setup_inputs():
    n = np.random.standard_normal
    s = mx_kscale(K)[:, None]
    u = mx_kscale(S)
    packed_xT = pack_weight(n((K, T)) * s)
    packed_w1 = pack_fp4(n((K, H)) / np.sqrt(K) / s)
    packed_dT = pack_weight(n((K, G)) / s)
    packed_w2 = pack_fp4(n((H, N)) / np.sqrt(2 * H) / u[:, None])
    packed_w3 = pack_fp4(n((H, N)) / np.sqrt(2 * H) / u[:, None])
    return {
        "x_words": packed_xT[0],
        "x_scales": packed_xT[1],
        "w1_words": packed_w1[0],
        "w1_scales": packed_w1[1],
        "d_words": packed_dT[0],
        "d_scales": packed_dT[1],
        "gn": (np.random.uniform(0.5, 1.5, (H, 1)) * u[:, None]).astype(np.float32),
        "gk": (np.random.uniform(0.5, 1.5, (H, 1)) * u[:, None]).astype(np.float32),
        "w2_words": packed_w2[0],
        "w2_scales": packed_w2[1],
        "w3_words": packed_w3[0],
        "w3_scales": packed_w3[1],
        "offs": striped(np.random.permutation(T)[:S]),
        "kidx": striped8(np.random.randint(0, G, (8, H))),
        "two": striped(np.random.permutation(T)[:S]),
        "n1": striped8(np.stack([np.random.permutation(S) for _ in range(8)])),
        "n2": striped8(np.stack([np.random.permutation(S) for _ in range(8)])),
        "n3": striped8(np.stack([np.random.permutation(S) for _ in range(8)])),
        "n4": striped(np.random.permutation(S)),
        "n5": striped(np.random.permutation(S)),
        "n6": striped(np.random.randint(0, S, W)),
    }


def reference(x_words, x_scales, w1_words, w1_scales, d_words, d_scales, gn, gk, w2_words, w2_scales, w3_words, w3_scales, offs, kidx, two, n1, n2, n3, n4, n5, n6):
    xq = unpack_weight(x_words, x_scales)[:, unstriped(offs)]
    y = unpack_fp4(w1_words, w1_scales).T @ xq
    z = f64(gn) * (np.maximum(y, y[np.arange(H)[:, None], runs(n1, H)]) - (np.maximum(y[np.arange(H)[:, None], runs(n2, H)], y[np.arange(H)[:, None], runs(n3, H)])))
    d_kidx = unpack_weight(d_words, d_scales)[np.arange(K)[:, None], runs(kidx, K)]
    x_two = unpack_weight(x_words, x_scales)[:, unstriped(two)]
    s = 0.0625 * (d_kidx.T @ x_two)
    st = s * (sigmoid(s[:, unstriped(n4)]))
    z2 = f64(gk) * (st - st[:, unstriped(n5)])
    h = unpack_fp4(w2_words, w2_scales).T @ mxq(z, 0, "e4m3") + unpack_fp4(w3_words, w3_scales).T @ mxq(z2, 0, "e4m3")
    mb = h[:, unstriped(n6)]
    ms = mb.reshape(N, S, 2).sum(axis=2)
    mx = mb.reshape(N, S, 2).max(axis=2)
    out_0 = ms - np.maximum(h, mx)
    return (out_0,) + planes(out_0)

@@ -1,0 +1,312 @@
+from contextlib import ExitStack
+
+import concourse.mybir as mybir
+
+K, T, S, N, H, G, W = 512, 1024, 512, 512, 512, 2048, 1024
+FLOPS = 4 * 2 * 512 * 512 * 512
+
+F32 = mybir.dt.float32
+BF16 = mybir.dt.bfloat16
+I32 = mybir.dt.int32
+U32 = mybir.dt.uint32
+U16 = mybir.dt.uint16
+U8 = mybir.dt.uint8
+FP8X4 = mybir.dt.float8_e4m3fn_x4
+FP4X4 = mybir.dt.float4_e2m1fn_x4
+ALU = mybir.AluOpType
+ACT = mybir.ActivationFunctionType
+
+P = 128
+PACK = 4
+CHUNKS = ((0, 256), (256, 384), (384, 512))
+SPARE = 16
+
+
+def tile_picked_jkeymixhopggpair_none_po_kernel(
+    tc, x_words, x_scales, w1_words, w1_scales, d_words, d_scales, gn, gk, w2_words, w2_scales, w3_words, w3_scales,
+    offs, kidx, two, n1, n2, n3, n4, n5, n6, out_0, out_1, out_2,
+):
+    nc = tc.nc
+    with ExitStack() as ctx:
+        keep = ctx.enter_context(tc.tile_pool(name="keep", bufs=1))
+        psum = ctx.enter_context(tc.psum_pool(name="psum", bufs=1))
+
+        def sb(name, shape, dtype, tag=None):
+            return keep.tile(shape, dtype, name=name, tag=tag or name, align_bytes=64)
+
+        def load_list(name, src):
+            t = keep.tile(list(src.shape), U16, name=name)
+            nc.sync.dma_start(t[:], src)
+            return t
+
+        def zeroed_bytes(name, width, engine):
+            t = sb(name, [P, width], U8)
+            engine.memset(t[:].bitcast(I32), 0)
+            return t
+
+        def load_scale_rows(name, src):
+            width = src.shape[2]
+            t = sb(name, [P, width], U8)
+            for q in range(4):
+                rows = src[:, 4 * q : 4 * q + 4, :].bitcast(I32)
+                nc.sync.dma_start(t[32 * q : 32 * q + 32, :].bitcast(I32), rows.to_broadcast([8, 4, width // 4]))
+            return t
+
+        def deal(engine, name, src, width, dtype):
+            t = sb(name, [P, 512 * width], dtype)
+            engine.tensor_copy(
+                t[:].rearrange("p (t m b) -> p t m b", t=PACK, b=width),
+                src.rearrange("p (m t b) -> p t m b", t=PACK, b=width),
+            )
+            return t
+
+        def gather(engine, out, window, offsets):
+            if engine is nc.scalar:
+                nc.scalar.activation(out, window.indirect(offsets), ACT.Copy)
+            else:
+                nc.vector.tensor_copy(out, window.indirect(offsets))
+
+        def evacuate(engine, out, bank):
+            if engine is nc.scalar:
+                nc.scalar.copy(out, bank)
+            else:
+                nc.vector.tensor_copy(out, bank)
+
+        def weave_in(planes, lo, hi):
+            return planes[:, :, lo:hi].rearrange("p t (c i) -> p c t i", i=4)
+
+        def weave_out(woven, lo, hi):
+            return woven[:, lo:hi, :].rearrange("p (c i) t -> p c t i", i=4)
+
+        ds_win = zeroed_bytes("ds_win", G, nc.vector)
+        ds_placed = zeroed_bytes("ds_placed", H, nc.gpsimd)
+
+        xw_win = sb("xw_win", [P, T], I32)
+        nc.sync.dma_start(xw_win[:], x_words[0].rearrange("p n t -> p (n t)").bitcast(I32))
+        offs_sb = load_list("offs_sb", offs)
+        xs_win = load_scale_rows("xs_win", x_scales)
+        w1w_raw = sb("w1w_raw", [P, 2 * H], U8)
+        nc.sync.dma_start(w1w_raw[:].bitcast(I32), w1_words[0].bitcast(I32))
+        w1s_raw = load_scale_rows("w1s_raw", w1_scales)
+        kidx_sb = load_list("kidx_sb", kidx)
+        nc.sync.dma_start(ds_win[0:P:8, :].bitcast(I32), d_scales[0].bitcast(I32))
+        n1_sb = load_list("n1_sb", n1)
+        n2_sb = load_list("n2_sb", n2)
+        n3_sb = load_list("n3_sb", n3)
+        two_sb = load_list("two_sb", two)
+        dw_win = sb("dw_win", [P, G], I32)
+        nc.sync.dma_start(dw_win[:], d_words[0].rearrange("p n t -> p (n t)").bitcast(I32))
+        gn_sb = sb("gn_sb", [P, PACK], F32)
+        nc.sync.dma_start(gn_sb[:], gn.rearrange("(p t) o -> p (t o)", t=PACK))
+        gk_sb = sb("gk_sb", [P, PACK], F32)
+        nc.sync.dma_start(gk_sb[:], gk.rearrange("(p t) o -> p (t o)", t=PACK))
+        n4_sb = load_list("n4_sb", n4)
+        n5_sb = load_list("n5_sb", n5)
+        n6_sb = load_list("n6_sb", n6)
+        w2w_raw = sb("w2w_raw", [P, 2 * N], U8)
+        nc.sync.dma_start(w2w_raw[:].bitcast(I32), w2_words[0].bitcast(I32))
+        w3w_raw = sb("w3w_raw", [P, 2 * N], U8)
+        nc.sync.dma_start(w3w_raw[:].bitcast(I32), w3_words[0].bitcast(I32))
+        w2s_raw = load_scale_rows("w2s_raw", w2_scales)
+        w3s_raw = load_scale_rows("w3s_raw", w3_scales)
+
+        y_win = [sb(f"y_win{t}", [P, 2 * S], F32) for t in range(PACK)]
+        sig_win = [sb(f"sig_win{t}", [P, S + SPARE], F32) for t in range(PACK)]
+        h_win = [sb(f"h_win{t}", [P, S + SPARE], F32) for t in range(PACK)]
+        for t in range(PACK):
+            nc.vector.memset(y_win[t][:, S:], 0.0)
+        for t in range(PACK):
+            nc.vector.memset(sig_win[t][:, S:], 0.0)
+            nc.vector.memset(h_win[t][:, S:], 0.0)
+
+        xw_offs = sb("xw_offs", [P, S], I32)
+        gather(nc.vector, xw_offs[:].bitcast(U32), xw_win[:].bitcast(U32), offs_sb[:])
+        xs_offs = sb("xs_offs", [P, S], U8)
+        gather(nc.vector, xs_offs[:], xs_win[:], offs_sb[:])
+        w1w = deal(nc.gpsimd, "w1w", w1w_raw[:], 2, U8)
+        w1s = deal(nc.gpsimd, "w1s", w1s_raw[:], 1, U8)
+        y_ps = [psum.tile([P, S], F32, name=f"y_ps{t}", tag=f"bank{t}") for t in range(PACK)]
+        for t in range(PACK):
+            nc.tensor.matmul_mx(
+                out=y_ps[t][:],
+                lhsT=w1w[:, 256 * t : 256 * (t + 1)].bitcast(FP4X4),
+                lhsT_scale=w1s[:, P * t : P * (t + 1)],
+                rhs=xw_offs[:].bitcast(FP8X4),
+                rhs_scale=xs_offs[:],
+                start=True,
+                stop=True,
+            )
+
+        ds_kidx = sb("ds_kidx", [P, H], U8)
+        gather(nc.vector, ds_kidx[:], ds_win[:], kidx_sb[:])
+        ds_dealt = deal(nc.vector, "ds_dealt", ds_kidx[:], 1, U8)
+        for q in range(4):
+            nc.sync.dma_start(
+                ds_placed[32 * q : 32 * q + 4, :].bitcast(I32), ds_dealt[32 * q : 32 * q + 32 : 8, :].bitcast(I32)
+            )
+        xw_two = sb("xw_two", [P, S], I32)
+        gather(nc.vector, xw_two[:].bitcast(U32), xw_win[:].bitcast(U32), two_sb[:])
+        xs_two = sb("xs_two", [P, S], U8)
+        gather(nc.vector, xs_two[:], xs_win[:], two_sb[:])
+        dw_kidx = sb("dw_kidx", [P, H], I32)
+        gather(nc.vector, dw_kidx[:].bitcast(U32), dw_win[:].bitcast(U32), kidx_sb[:])
+        dw = deal(nc.vector, "dw", dw_kidx[:], 1, I32)
+        s_ps = [psum.tile([P, S], F32, name=f"s_ps{t}", tag=f"bank{PACK + t}") for t in range(PACK)]
+        for t in range(PACK):
+            nc.tensor.matmul_mx(
+                out=s_ps[t][:],
+                lhsT=dw[:, P * t : P * (t + 1)].bitcast(FP8X4),
+                lhsT_scale=ds_placed[:, P * t : P * (t + 1)],
+                rhs=xw_two[:].bitcast(FP8X4),
+                rhs_scale=xs_two[:],
+                start=True,
+                stop=True,
+            )
+
+        w2w = deal(nc.gpsimd, "w2w", w2w_raw[:], 2, U8)
+        w3w = deal(nc.gpsimd, "w3w", w3w_raw[:], 2, U8)
+        w2s = deal(nc.gpsimd, "w2s", w2s_raw[:], 1, U8)
+        w3s = deal(nc.gpsimd, "w3s", w3s_raw[:], 1, U8)
+        gk16 = sb("gk16", [P, PACK], F32)
+        nc.vector.tensor_scalar(gk16[:], gk_sb[:], 0.0625, None, ALU.mult)
+
+        on_vector = ((2, 0), (2, 1), (2, 2), (3, 0))
+        after_d = sb("after_d", [P, 12, S], F32, tag="dw_win")
+        y_at = [
+            [
+                after_d[:, 8 + on_vector.index((t, i)), :] if (t, i) in on_vector else sb(f"y_at{t}_{i}", [P, S], F32)[:]
+                for i in range(3)
+            ]
+            for t in range(PACK)
+        ]
+        top1 = [after_d[:, t, :] for t in range(PACK)]
+        top2 = [after_d[:, PACK + t, :] for t in range(PACK)]
+        gap = sb("gap", [P, PACK, S], F32)
+        y_lists = (n1_sb, n2_sb, n3_sb)
+
+        def y_gathers(t):
+            evacuate(nc.scalar, y_win[t][:, :S], y_ps[t][:])
+            for i in range(3):
+                engine = nc.vector if (t, i) in on_vector else nc.scalar
+                gather(engine, y_at[t][i], y_win[t][:], y_lists[i][:])
+
+        def y_tops(t):
+            nc.vector.tensor_tensor(top1[t], y_at[t][0], y_ps[t][:], ALU.max)
+            nc.vector.tensor_tensor(top2[t], y_at[t][1], y_at[t][2], ALU.max)
+
+        def y_gap(t):
+            nc.vector.tensor_tensor(gap[:, t, :], top1[t], top2[t], ALU.subtract)
+
+        y_gathers(0)
+        y_gathers(2)
+        y_gathers(1)
+        y_tops(0)
+        y_gathers(3)
+        y_gap(0)
+        y_tops(2)
+        y_tops(1)
+        y_gap(2)
+        y_gap(1)
+        y_tops(3)
+
+        sig_at = [sb(f"sig_at{t}", [P, S], F32) for t in range(PACK)]
+        st = sb("st", [P, PACK, S], F32)
+        st_at = sb("st_at", [P, PACK, S], F32)
+
+        def s_gate(t):
+            nc.scalar.activation(sig_win[t][:, :S], s_ps[t][:], ACT.Sigmoid, scale=0.0625)
+            gather(nc.scalar, sig_at[t][:], sig_win[t][:], n4_sb[:])
+            nc.vector.scalar_tensor_tensor(
+                st[:, t, :], s_ps[t][:], gk16[:, t : t + 1], sig_at[t][:], ALU.mult, ALU.mult
+            )
+
+        s_gate(0)
+        y_gap(3)
+        s_gate(1)
+        z_bf = sb("z_bf", [P, S, PACK], BF16)
+        nc.vector.tensor_tensor(
+            weave_out(z_bf, 0, S),
+            weave_in(gap, 0, S),
+            gn_sb[:].unsqueeze(1).unsqueeze(3).to_broadcast([P, S // 4, PACK, 4]),
+            ALU.mult,
+        )
+        s_gate(2)
+        z_w = sb("z_w", [P, S], I32)
+        z_s = sb("z_s", [P, S], U8)
+        nc.vector.quantize_mx(out=z_w[:].bitcast(FP8X4), scales=z_s[:], in_=z_bf[:].rearrange("p j t -> p (j t)"))
+        s_gate(3)
+
+        h_ps = [psum.tile([P, S], F32, name=f"h_ps{t}", tag=f"bank{t}") for t in range(PACK)]
+        for t in range(PACK):
+            nc.tensor.matmul_mx(
+                out=h_ps[t][:],
+                lhsT=w2w[:, 256 * t : 256 * (t + 1)].bitcast(FP4X4),
+                lhsT_scale=w2s[:, P * t : P * (t + 1)],
+                rhs=z_w[:].bitcast(FP8X4),
+                rhs_scale=z_s[:],
+                start=True,
+                stop=False,
+            )
+
+        z2_bf = sb("z2_bf", [P, S, PACK], BF16)
+        z2_w = sb("z2_w", [P, S], I32)
+        z2_s = sb("z2_s", [P, S], U8)
+        for lo, hi in CHUNKS:
+            for t in range(PACK):
+                gather(nc.scalar, st_at[:, t, lo:hi], st[:, t, :], n5_sb[:, lo // 16 : hi // 16])
+            nc.vector.tensor_tensor(weave_out(z2_bf, lo, hi), weave_in(st, lo, hi), weave_in(st_at, lo, hi), ALU.subtract)
+            nc.vector.quantize_mx(
+                out=z2_w[:, lo:hi].bitcast(FP8X4),
+                scales=z2_s[:, lo:hi],
+                in_=z2_bf[:, lo:hi, :].rearrange("p j t -> p (j t)"),
+            )
+            for t in range(PACK):
+                nc.tensor.matmul_mx(
+                    out=h_ps[t][:, lo:hi],
+                    lhsT=w3w[:, 256 * t : 256 * (t + 1)].bitcast(FP4X4),
+                    lhsT_scale=w3s[:, P * t : P * (t + 1)],
+                    rhs=z2_w[:, lo:hi].bitcast(FP8X4),
+                    rhs_scale=z2_s[:, lo:hi],
+                    start=False,
+                    stop=(hi == S),
+                )
+
+        for t in range(PACK):
+            evacuate(nc.scalar if t == 0 else nc.vector, h_win[t][:, :S], h_ps[t][:])
+        members = [sb(f"members{t}", [P, S, 2], F32) for t in range(PACK)]
+        under = [sb(f"under{t}", [P, S], F32) for t in range(PACK)]
+        left = [sb(f"left{t}", [P, S], F32) for t in range(PACK)]
+        res = sb("res", [P, PACK, S], F32)
+        res_bf = sb("res_bf", [P, S, PACK], BF16)
+        res_w = sb("res_w", [P, S], I32)
+        res_s = sb("res_s", [P, S], U8)
+        out_rows = out_0.rearrange("(p t) j -> p t j", t=PACK)
+        out_words = out_1[0].rearrange("p n t -> p (n t)").bitcast(I32)
+        for lo, hi in CHUNKS:
+            for t in range(PACK):
+                gather(
+                    nc.scalar,
+                    members[t][:, lo:hi, :].rearrange("p j e -> p (j e)"),
+                    h_win[t][:],
+                    n6_sb[:, lo // 8 : hi // 8],
+                )
+            for pair in ((0, 1), (2, 3)):
+                for t in pair:
+                    nc.vector.tensor_tensor(under[t][:, lo:hi], members[t][:, lo:hi, 1], h_ps[t][:, lo:hi], ALU.subtract)
+                for t in pair:
+                    nc.vector.scalar_tensor_tensor(
+                        left[t][:, lo:hi], under[t][:, lo:hi], 0.0, members[t][:, lo:hi, 0], ALU.min, ALU.add
+                    )
+                for t in pair:
+                    nc.vector.tensor_tensor(res[:, t, lo:hi], left[t][:, lo:hi], members[t][:, lo:hi, 1], ALU.min)
+            nc.sync.dma_start(out_rows[:, :, lo:hi], res[:, :, lo:hi])
+            nc.vector.tensor_copy(weave_out(res_bf, lo, hi), weave_in(res, lo, hi))
+            nc.vector.quantize_mx(
+                out=res_w[:, lo:hi].bitcast(FP8X4),
+                scales=res_s[:, lo:hi],
+                in_=res_bf[:, lo:hi, :].rearrange("p j t -> p (j t)"),
+            )
+            nc.sync.dma_start(out_words[:, lo:hi], res_w[:, lo:hi])
+        for q in range(4):
+            queue = nc.scalar if q % 2 else nc.sync
+            queue.dma_start(out_2[0, 4 * q : 4 * q + 4, :].bitcast(I32), res_s[32 * q : 32 * q + 4, :].bitcast(I32))

@@ -19,6 +19,12 @@ ACT = mybir.ActivationFunctionType
 P = 128
 PACK = 4
 CHUNKS = ((0, 256), (256, 384), (384, 512))
+OUT_CHUNKS = ((0, 256), (256, 384), (384, 512))
+OUT_ON_VECTOR = ((0, 1),)
+H_ON_SCALAR = (0, 2)
+ROUND_ON_SCALAR = (256,)
+Y_OUT_ON_VECTOR = ()
+Y_AT_ON_VECTOR = ((2, 0), (2, 1), (2, 2), (3, 0))
 SPARE = 16
 
 
@@ -44,18 +50,17 @@ def tile_picked_jkeymixhopggpair_none_po_kernel(
             engine.memset(t[:].bitcast(I32), 0)
             return t
 
-        def load_scale_rows(name, src):
+        def load_scale_rows(name, src, queues):
             width = src.shape[2]
             t = sb(name, [P, width], U8)
             for q in range(4):
                 rows = src[:, 4 * q : 4 * q + 4, :].bitcast(I32)
-                nc.sync.dma_start(t[32 * q : 32 * q + 32, :].bitcast(I32), rows.to_broadcast([8, 4, width // 4]))
+                queues[q].dma_start(t[32 * q : 32 * q + 32, :].bitcast(I32), rows.to_broadcast([8, 4, width // 4]))
             return t
 
-        def deal(engine, name, src, width, dtype):
-            t = sb(name, [P, 512 * width], dtype)
+        def deal(engine, t, src, width):
             engine.tensor_copy(
-                t[:].rearrange("p (t m b) -> p t m b", t=PACK, b=width),
+                t.rearrange("p (t m b) -> p t m b", t=PACK, b=width),
                 src.rearrange("p (m t b) -> p t m b", t=PACK, b=width),
             )
             return t
@@ -78,24 +83,34 @@ def tile_picked_jkeymixhopggpair_none_po_kernel(
         def weave_out(woven, lo, hi):
             return woven[:, lo:hi, :].rearrange("p (c i) t -> p c t i", i=4)
 
+        warm = sb("warm", [P, 2], F32)
+        nc.vector.memset(warm[:, 0:1], 0.0)
+        nc.scalar.activation(warm[:, 1:2], warm[:, 0:1], ACT.Sigmoid)
         ds_win = zeroed_bytes("ds_win", G, nc.vector)
-        ds_placed = zeroed_bytes("ds_placed", H, nc.gpsimd)
+        ds_placed = zeroed_bytes("ds_placed", H, nc.vector)
 
-        xw_win = sb("xw_win", [P, T], I32)
-        nc.sync.dma_start(xw_win[:], x_words[0].rearrange("p n t -> p (n t)").bitcast(I32))
+        on_sync = [nc.sync] * 4
         offs_sb = load_list("offs_sb", offs)
-        xs_win = load_scale_rows("xs_win", x_scales)
+        xs_win = load_scale_rows("xs_win", x_scales, on_sync)
         w1w_raw = sb("w1w_raw", [P, 2 * H], U8)
         nc.sync.dma_start(w1w_raw[:].bitcast(I32), w1_words[0].bitcast(I32))
-        w1s_raw = load_scale_rows("w1s_raw", w1_scales)
+        xw_win = sb("xw_win", [P, T], I32)
+        nc.sync.dma_start(xw_win[:], x_words[0].rearrange("p n t -> p (n t)").bitcast(I32))
+        w1s_raw = load_scale_rows("w1s_raw", w1_scales, on_sync)
+        two_sb = load_list("two_sb", two)
         kidx_sb = load_list("kidx_sb", kidx)
         nc.sync.dma_start(ds_win[0:P:8, :].bitcast(I32), d_scales[0].bitcast(I32))
         n1_sb = load_list("n1_sb", n1)
         n2_sb = load_list("n2_sb", n2)
         n3_sb = load_list("n3_sb", n3)
-        two_sb = load_list("two_sb", two)
+        w2w_raw = sb("w2w_raw", [P, 2 * N], U8)
+        nc.sync.dma_start(w2w_raw[:].bitcast(I32), w2_words[0].bitcast(I32))
+        w3w_raw = sb("w3w_raw", [P, 2 * N], U8)
+        nc.sync.dma_start(w3w_raw[:].bitcast(I32), w3_words[0].bitcast(I32))
         dw_win = sb("dw_win", [P, G], I32)
         nc.sync.dma_start(dw_win[:], d_words[0].rearrange("p n t -> p (n t)").bitcast(I32))
+        w2s_raw = load_scale_rows("w2s_raw", w2_scales, on_sync)
+        w3s_raw = load_scale_rows("w3s_raw", w3_scales, on_sync)
         gn_sb = sb("gn_sb", [P, PACK], F32)
         nc.sync.dma_start(gn_sb[:], gn.rearrange("(p t) o -> p (t o)", t=PACK))
         gk_sb = sb("gk_sb", [P, PACK], F32)
@@ -103,28 +118,17 @@ def tile_picked_jkeymixhopggpair_none_po_kernel(
         n4_sb = load_list("n4_sb", n4)
         n5_sb = load_list("n5_sb", n5)
         n6_sb = load_list("n6_sb", n6)
-        w2w_raw = sb("w2w_raw", [P, 2 * N], U8)
-        nc.sync.dma_start(w2w_raw[:].bitcast(I32), w2_words[0].bitcast(I32))
-        w3w_raw = sb("w3w_raw", [P, 2 * N], U8)
-        nc.sync.dma_start(w3w_raw[:].bitcast(I32), w3_words[0].bitcast(I32))
-        w2s_raw = load_scale_rows("w2s_raw", w2_scales)
-        w3s_raw = load_scale_rows("w3s_raw", w3_scales)
 
         y_win = [sb(f"y_win{t}", [P, 2 * S], F32) for t in range(PACK)]
         sig_win = [sb(f"sig_win{t}", [P, S + SPARE], F32) for t in range(PACK)]
         h_win = [sb(f"h_win{t}", [P, S + SPARE], F32) for t in range(PACK)]
-        for t in range(PACK):
-            nc.vector.memset(y_win[t][:, S:], 0.0)
-        for t in range(PACK):
-            nc.vector.memset(sig_win[t][:, S:], 0.0)
-            nc.vector.memset(h_win[t][:, S:], 0.0)
 
-        xw_offs = sb("xw_offs", [P, S], I32)
-        gather(nc.vector, xw_offs[:].bitcast(U32), xw_win[:].bitcast(U32), offs_sb[:])
         xs_offs = sb("xs_offs", [P, S], U8)
         gather(nc.vector, xs_offs[:], xs_win[:], offs_sb[:])
-        w1w = deal(nc.gpsimd, "w1w", w1w_raw[:], 2, U8)
-        w1s = deal(nc.gpsimd, "w1s", w1s_raw[:], 1, U8)
+        xw_offs = sb("xw_offs", [P, S], I32)
+        gather(nc.vector, xw_offs[:].bitcast(U32), xw_win[:].bitcast(U32), offs_sb[:])
+        w1w = deal(nc.gpsimd, sb("w1w", [P, 2 * H], U8)[:], w1w_raw[:], 2)
+        w1s = deal(nc.gpsimd, sb("w1s", [P, H], U8)[:], w1s_raw[:], 1)
         y_ps = [psum.tile([P, S], F32, name=f"y_ps{t}", tag=f"bank{t}") for t in range(PACK)]
         for t in range(PACK):
             nc.tensor.matmul_mx(
@@ -139,7 +143,7 @@ def tile_picked_jkeymixhopggpair_none_po_kernel(
 
         ds_kidx = sb("ds_kidx", [P, H], U8)
         gather(nc.vector, ds_kidx[:], ds_win[:], kidx_sb[:])
-        ds_dealt = deal(nc.vector, "ds_dealt", ds_kidx[:], 1, U8)
+        ds_dealt = deal(nc.vector, sb("ds_dealt", [P, H], U8)[:], ds_kidx[:], 1)
         for q in range(4):
             nc.sync.dma_start(
                 ds_placed[32 * q : 32 * q + 4, :].bitcast(I32), ds_dealt[32 * q : 32 * q + 32 : 8, :].bitcast(I32)
@@ -150,7 +154,7 @@ def tile_picked_jkeymixhopggpair_none_po_kernel(
         gather(nc.vector, xs_two[:], xs_win[:], two_sb[:])
         dw_kidx = sb("dw_kidx", [P, H], I32)
         gather(nc.vector, dw_kidx[:].bitcast(U32), dw_win[:].bitcast(U32), kidx_sb[:])
-        dw = deal(nc.vector, "dw", dw_kidx[:], 1, I32)
+        dw = deal(nc.vector, sb("dw", [P, H], I32)[:], dw_kidx[:], 1)
         s_ps = [psum.tile([P, S], F32, name=f"s_ps{t}", tag=f"bank{PACK + t}") for t in range(PACK)]
         for t in range(PACK):
             nc.tensor.matmul_mx(
@@ -163,15 +167,16 @@ def tile_picked_jkeymixhopggpair_none_po_kernel(
                 stop=True,
             )
 
-        w2w = deal(nc.gpsimd, "w2w", w2w_raw[:], 2, U8)
-        w3w = deal(nc.gpsimd, "w3w", w3w_raw[:], 2, U8)
-        w2s = deal(nc.gpsimd, "w2s", w2s_raw[:], 1, U8)
-        w3s = deal(nc.gpsimd, "w3s", w3s_raw[:], 1, U8)
+        w23 = sb("w23", [P, 6 * N], U8, tag="dw_kidx")
+        w2w = deal(nc.gpsimd, w23[:, 0 : 2 * N], w2w_raw[:], 2)
+        w2s = deal(nc.gpsimd, w23[:, 4 * N : 5 * N], w2s_raw[:], 1)
+        w3w = deal(nc.gpsimd, w23[:, 2 * N : 4 * N], w3w_raw[:], 2)
+        w3s = deal(nc.gpsimd, w23[:, 5 * N : 6 * N], w3s_raw[:], 1)
         gk16 = sb("gk16", [P, PACK], F32)
         nc.vector.tensor_scalar(gk16[:], gk_sb[:], 0.0625, None, ALU.mult)
 
-        on_vector = ((2, 0), (2, 1), (2, 2), (3, 0))
-        after_d = sb("after_d", [P, 12, S], F32, tag="dw_win")
+        on_vector = Y_AT_ON_VECTOR
+        after_d = sb("after_d", [P, 8 + len(on_vector), S], F32, tag="dw_win")
         y_at = [
             [
                 after_d[:, 8 + on_vector.index((t, i)), :] if (t, i) in on_vector else sb(f"y_at{t}_{i}", [P, S], F32)[:]
@@ -184,8 +189,10 @@ def tile_picked_jkeymixhopggpair_none_po_kernel(
         gap = sb("gap", [P, PACK, S], F32)
         y_lists = (n1_sb, n2_sb, n3_sb)
 
+        def y_out(t):
+            evacuate(nc.vector if t in Y_OUT_ON_VECTOR else nc.scalar, y_win[t][:, :S], y_ps[t][:])
+
         def y_gathers(t):
-            evacuate(nc.scalar, y_win[t][:, :S], y_ps[t][:])
             for i in range(3):
                 engine = nc.vector if (t, i) in on_vector else nc.scalar
                 gather(engine, y_at[t][i], y_win[t][:], y_lists[i][:])
@@ -197,13 +204,17 @@ def tile_picked_jkeymixhopggpair_none_po_kernel(
         def y_gap(t):
             nc.vector.tensor_tensor(gap[:, t, :], top1[t], top2[t], ALU.subtract)
 
-        y_gathers(0)
+        y_out(0)
+        y_out(2)
         y_gathers(2)
-        y_gathers(1)
+        y_gathers(0)
         y_tops(0)
-        y_gathers(3)
-        y_gap(0)
+        y_out(1)
+        y_gathers(1)
         y_tops(2)
+        y_gap(0)
+        y_out(3)
+        y_gathers(3)
         y_tops(1)
         y_gap(2)
         y_gap(1)
@@ -211,7 +222,6 @@ def tile_picked_jkeymixhopggpair_none_po_kernel(
 
         sig_at = [sb(f"sig_at{t}", [P, S], F32) for t in range(PACK)]
         st = sb("st", [P, PACK, S], F32)
-        st_at = sb("st_at", [P, PACK, S], F32)
 
         def s_gate(t):
             nc.scalar.activation(sig_win[t][:, :S], s_ps[t][:], ACT.Sigmoid, scale=0.0625)
@@ -220,20 +230,25 @@ def tile_picked_jkeymixhopggpair_none_po_kernel(
                 st[:, t, :], s_ps[t][:], gk16[:, t : t + 1], sig_at[t][:], ALU.mult, ALU.mult
             )
 
-        s_gate(0)
-        y_gap(3)
-        s_gate(1)
         z_bf = sb("z_bf", [P, S, PACK], BF16)
-        nc.vector.tensor_tensor(
-            weave_out(z_bf, 0, S),
-            weave_in(gap, 0, S),
-            gn_sb[:].unsqueeze(1).unsqueeze(3).to_broadcast([P, S // 4, PACK, 4]),
-            ALU.mult,
-        )
-        s_gate(2)
+
+        def z_half(lo, hi):
+            nc.vector.tensor_tensor(
+                weave_out(z_bf, lo, hi),
+                weave_in(gap, lo, hi),
+                gn_sb[:].unsqueeze(1).unsqueeze(3).to_broadcast([P, (hi - lo) // 4, PACK, 4]),
+                ALU.mult,
+            )
+
         z_w = sb("z_w", [P, S], I32)
         z_s = sb("z_s", [P, S], U8)
+        y_gap(3)
+        z_half(0, S // 2)
+        s_gate(0)
+        z_half(S // 2, S)
+        s_gate(1)
         nc.vector.quantize_mx(out=z_w[:].bitcast(FP8X4), scales=z_s[:], in_=z_bf[:].rearrange("p j t -> p (j t)"))
+        s_gate(2)
         s_gate(3)
 
         h_ps = [psum.tile([P, S], F32, name=f"h_ps{t}", tag=f"bank{t}") for t in range(PACK)]
@@ -248,63 +263,64 @@ def tile_picked_jkeymixhopggpair_none_po_kernel(
                 stop=False,
             )
 
-        z2_bf = sb("z2_bf", [P, S, PACK], BF16)
-        z2_w = sb("z2_w", [P, S], I32)
-        z2_s = sb("z2_s", [P, S], U8)
         for lo, hi in CHUNKS:
+            n = hi - lo
+            st_at = sb(f"st_at{lo}", [P, PACK, n], F32)
+            z2_bf = sb(f"z2_bf{lo}", [P, n, PACK], BF16)
+            z2_w = sb(f"z2_w{lo}", [P, n], I32)
+            z2_s = sb(f"z2_s{lo}", [P, n], U8)
             for t in range(PACK):
-                gather(nc.scalar, st_at[:, t, lo:hi], st[:, t, :], n5_sb[:, lo // 16 : hi // 16])
-            nc.vector.tensor_tensor(weave_out(z2_bf, lo, hi), weave_in(st, lo, hi), weave_in(st_at, lo, hi), ALU.subtract)
-            nc.vector.quantize_mx(
-                out=z2_w[:, lo:hi].bitcast(FP8X4),
-                scales=z2_s[:, lo:hi],
-                in_=z2_bf[:, lo:hi, :].rearrange("p j t -> p (j t)"),
-            )
+                window = st[:, t, :] if lo == 0 else st[:, t:, :].rearrange("p t j -> p (t j)")
+                gather(nc.scalar, st_at[:, t, :], window, n5_sb[:, lo // 16 : hi // 16])
+            nc.vector.tensor_tensor(weave_out(z2_bf, 0, n), weave_in(st, lo, hi), weave_in(st_at, 0, n), ALU.subtract)
+            nc.vector.quantize_mx(out=z2_w[:].bitcast(FP8X4), scales=z2_s[:], in_=z2_bf[:].rearrange("p j t -> p (j t)"))
             for t in range(PACK):
                 nc.tensor.matmul_mx(
                     out=h_ps[t][:, lo:hi],
                     lhsT=w3w[:, 256 * t : 256 * (t + 1)].bitcast(FP4X4),
                     lhsT_scale=w3s[:, P * t : P * (t + 1)],
-                    rhs=z2_w[:, lo:hi].bitcast(FP8X4),
-                    rhs_scale=z2_s[:, lo:hi],
+                    rhs=z2_w[:].bitcast(FP8X4),
+                    rhs_scale=z2_s[:],
                     start=False,
                     stop=(hi == S),
                 )
 
         for t in range(PACK):
-            evacuate(nc.scalar if t == 0 else nc.vector, h_win[t][:, :S], h_ps[t][:])
-        members = [sb(f"members{t}", [P, S, 2], F32) for t in range(PACK)]
-        under = [sb(f"under{t}", [P, S], F32) for t in range(PACK)]
-        left = [sb(f"left{t}", [P, S], F32) for t in range(PACK)]
-        res = sb("res", [P, PACK, S], F32)
-        res_bf = sb("res_bf", [P, S, PACK], BF16)
+            evacuate(nc.scalar if t in H_ON_SCALAR else nc.vector, h_win[t][:, :S], h_ps[t][:])
         res_w = sb("res_w", [P, S], I32)
         res_s = sb("res_s", [P, S], U8)
         out_rows = out_0.rearrange("(p t) j -> p t j", t=PACK)
         out_words = out_1[0].rearrange("p n t -> p (n t)").bitcast(I32)
-        for lo, hi in CHUNKS:
+        all_members = {}
+        for lo, hi in OUT_CHUNKS:
+            members = [sb(f"members{lo}_{u}", [P, 2, hi - lo, 2], F32) for u in range(2)]
+            all_members[lo] = members
             for t in range(PACK):
                 gather(
-                    nc.scalar,
-                    members[t][:, lo:hi, :].rearrange("p j e -> p (j e)"),
+                    nc.vector if (lo, t) in OUT_ON_VECTOR else nc.scalar,
+                    members[t // 2][:, t % 2, :, :].rearrange("p j e -> p (j e)"),
                     h_win[t][:],
                     n6_sb[:, lo // 8 : hi // 8],
                 )
-            for pair in ((0, 1), (2, 3)):
-                for t in pair:
-                    nc.vector.tensor_tensor(under[t][:, lo:hi], members[t][:, lo:hi, 1], h_ps[t][:, lo:hi], ALU.subtract)
-                for t in pair:
-                    nc.vector.scalar_tensor_tensor(
-                        left[t][:, lo:hi], under[t][:, lo:hi], 0.0, members[t][:, lo:hi, 0], ALU.min, ALU.add
-                    )
-                for t in pair:
-                    nc.vector.tensor_tensor(res[:, t, lo:hi], left[t][:, lo:hi], members[t][:, lo:hi, 1], ALU.min)
-            nc.sync.dma_start(out_rows[:, :, lo:hi], res[:, :, lo:hi])
-            nc.vector.tensor_copy(weave_out(res_bf, lo, hi), weave_in(res, lo, hi))
+        for lo, hi in OUT_CHUNKS:
+            n = hi - lo
+            members = all_members[lo]
+            under = sb(f"under{lo}", [P, PACK, n], F32)
+            left = sb(f"left{lo}", [P, PACK, n], F32)
+            res = sb(f"res{lo}", [P, PACK, n], F32)
+            res_bf = sb(f"res_bf{lo}", [P, n, PACK], BF16)
+            for t in range(PACK):
+                nc.vector.tensor_tensor(under[:, t, :], members[t // 2][:, t % 2, :, 1], h_ps[t][:, lo:hi], ALU.subtract)
+            for u in range(2):
+                pair = slice(2 * u, 2 * u + 2)
+                nc.vector.scalar_tensor_tensor(left[:, pair, :], under[:, pair, :], 0.0, members[u][:, :, :, 0], ALU.min, ALU.add)
+            for u in range(2):
+                pair = slice(2 * u, 2 * u + 2)
+                nc.vector.tensor_tensor(res[:, pair, :], left[:, pair, :], members[u][:, :, :, 1], ALU.min)
+            nc.sync.dma_start(out_rows[:, :, lo:hi], res[:])
+            evacuate(nc.scalar if lo in ROUND_ON_SCALAR else nc.vector, weave_out(res_bf, 0, n), weave_in(res, 0, n))
             nc.vector.quantize_mx(
-                out=res_w[:, lo:hi].bitcast(FP8X4),
-                scales=res_s[:, lo:hi],
-                in_=res_bf[:, lo:hi, :].rearrange("p j t -> p (j t)"),
+                out=res_w[:, lo:hi].bitcast(FP8X4), scales=res_s[:, lo:hi], in_=res_bf[:].rearrange("p j t -> p (j t)")
             )
             nc.sync.dma_start(out_words[:, lo:hi], res_w[:, lo:hi])
         for q in range(4):

@@ -2,7 +2,7 @@ from contextlib import ExitStack
 
 import concourse.mybir as mybir
 
-K, T, S, N, H, G, W = 512, 1024, 512, 512, 512, 2048, 1024
+S, N, H, G = 512, 512, 512, 2048
 FLOPS = 4 * 2 * 512 * 512 * 512
 
 F32 = mybir.dt.float32
@@ -17,15 +17,13 @@ ALU = mybir.AluOpType
 ACT = mybir.ActivationFunctionType
 
 P = 128
-PACK = 4
-CHUNKS = ((0, 256), (256, 384), (384, 512))
-OUT_CHUNKS = ((0, 256), (256, 384), (384, 512))
-OUT_ON_VECTOR = ((0, 1),)
-H_ON_SCALAR = (0, 2)
-ROUND_ON_SCALAR = (256,)
-Y_OUT_ON_VECTOR = ()
-Y_AT_ON_VECTOR = ((2, 0), (2, 1), (2, 2), (3, 0))
+PLANES = 4
+HALF = S // 2
+FIRST, MIDDLE, LAST = 0, 256, 384
+CHUNKS = ((FIRST, MIDDLE), (MIDDLE, LAST), (LAST, S))
 SPARE = 16
+Y_LOOKUPS_ON_VECTOR = ((2, 0), (2, 1), (2, 2), (3, 0))
+H_LOOKUPS_ON_VECTOR = ((FIRST, 1), (MIDDLE, 1))
 
 
 def tile_picked_jkeymixhopggpair_none_po_kernel(
@@ -41,122 +39,133 @@ def tile_picked_jkeymixhopggpair_none_po_kernel(
             return keep.tile(shape, dtype, name=name, tag=tag or name, align_bytes=64)
 
         def load_list(name, src):
-            t = keep.tile(list(src.shape), U16, name=name)
-            nc.sync.dma_start(t[:], src)
-            return t
+            tile = keep.tile(list(src.shape), U16, name=name)
+            nc.sync.dma_start(tile[:], src)
+            return tile
 
-        def zeroed_bytes(name, width, engine):
-            t = sb(name, [P, width], U8)
-            engine.memset(t[:].bitcast(I32), 0)
-            return t
+        def load_fp8_words(name, src):
+            tile = sb(name, [P, src.shape[2]], I32)
+            nc.sync.dma_start(tile[:], src[0].rearrange("p n t -> p (n t)").bitcast(I32))
+            return tile
 
-        def load_scale_rows(name, src, queues):
+        def load_fp4_words(name, src):
+            tile = sb(name, [P, src.shape[2]], U8)
+            nc.sync.dma_start(tile[:].bitcast(I32), src[0].bitcast(I32))
+            return tile
+
+        def load_scale_rows(name, src):
             width = src.shape[2]
-            t = sb(name, [P, width], U8)
+            tile = sb(name, [P, width], U8)
             for q in range(4):
                 rows = src[:, 4 * q : 4 * q + 4, :].bitcast(I32)
-                queues[q].dma_start(t[32 * q : 32 * q + 32, :].bitcast(I32), rows.to_broadcast([8, 4, width // 4]))
-            return t
+                nc.sync.dma_start(tile[32 * q : 32 * q + 32, :].bitcast(I32), rows.to_broadcast([8, 4, width // 4]))
+            return tile
 
-        def deal(engine, t, src, width):
+        def load_gain(name, src):
+            tile = sb(name, [P, PLANES], F32)
+            nc.sync.dma_start(tile[:], src.rearrange("(p t) o -> p (t o)", t=PLANES))
+            return tile
+
+        def zeroed_bytes(name, width):
+            tile = sb(name, [P, width], U8)
+            nc.vector.memset(tile[:].bitcast(I32), 0)
+            return tile
+
+        def deal(engine, dealt, src, per_column=1):
             engine.tensor_copy(
-                t.rearrange("p (t m b) -> p t m b", t=PACK, b=width),
-                src.rearrange("p (m t b) -> p t m b", t=PACK, b=width),
+                dealt.rearrange("p (t m b) -> p t m b", t=PLANES, b=per_column),
+                src.rearrange("p (m t b) -> p t m b", t=PLANES, b=per_column),
             )
-            return t
+            return dealt
 
-        def gather(engine, out, window, offsets):
-            if engine is nc.scalar:
-                nc.scalar.activation(out, window.indirect(offsets), ACT.Copy)
-            else:
+        def gather(on_vector, out, window, offsets):
+            if on_vector:
                 nc.vector.tensor_copy(out, window.indirect(offsets))
-
-        def evacuate(engine, out, bank):
-            if engine is nc.scalar:
-                nc.scalar.copy(out, bank)
             else:
-                nc.vector.tensor_copy(out, bank)
+                nc.scalar.activation(out, window.indirect(offsets), ACT.Copy)
 
-        def weave_in(planes, lo, hi):
-            return planes[:, :, lo:hi].rearrange("p t (c i) -> p c t i", i=4)
+        def plain_copy(on_vector, out, src):
+            if on_vector:
+                nc.vector.tensor_copy(out, src)
+            else:
+                nc.scalar.copy(out, src)
 
-        def weave_out(woven, lo, hi):
-            return woven[:, lo:hi, :].rearrange("p (c i) t -> p c t i", i=4)
+        def weave_in(planes):
+            return planes.rearrange("p t (c i) -> p c t i", i=4)
+
+        def weave_out(woven):
+            return woven.rearrange("p (c i) t -> p c t i", i=4)
+
+        def quantize(words, scales, woven):
+            nc.vector.quantize_mx(out=words.bitcast(FP8X4), scales=scales, in_=woven.rearrange("p j t -> p (j t)"))
+
+        def fp4_pass(out, t, w_words, w_scales, words, scales, start, stop):
+            nc.tensor.matmul_mx(
+                out=out,
+                lhsT=w_words[:, 2 * P * t : 2 * P * (t + 1)].bitcast(FP4X4),
+                lhsT_scale=w_scales[:, P * t : P * (t + 1)],
+                rhs=words.bitcast(FP8X4),
+                rhs_scale=scales,
+                start=start,
+                stop=stop,
+            )
 
         warm = sb("warm", [P, 2], F32)
         nc.vector.memset(warm[:, 0:1], 0.0)
         nc.scalar.activation(warm[:, 1:2], warm[:, 0:1], ACT.Sigmoid)
-        ds_win = zeroed_bytes("ds_win", G, nc.vector)
-        ds_placed = zeroed_bytes("ds_placed", H, nc.vector)
 
-        on_sync = [nc.sync] * 4
+        ds_win = zeroed_bytes("ds_win", G)
+        ds_placed = zeroed_bytes("ds_placed", H)
+        w1w_raw = load_fp4_words("w1w_raw", w1_words)
         offs_sb = load_list("offs_sb", offs)
-        xs_win = load_scale_rows("xs_win", x_scales, on_sync)
-        w1w_raw = sb("w1w_raw", [P, 2 * H], U8)
-        nc.sync.dma_start(w1w_raw[:].bitcast(I32), w1_words[0].bitcast(I32))
-        xw_win = sb("xw_win", [P, T], I32)
-        nc.sync.dma_start(xw_win[:], x_words[0].rearrange("p n t -> p (n t)").bitcast(I32))
-        w1s_raw = load_scale_rows("w1s_raw", w1_scales, on_sync)
+        xs_win = load_scale_rows("xs_win", x_scales)
+        xw_win = load_fp8_words("xw_win", x_words)
+        w1s_raw = load_scale_rows("w1s_raw", w1_scales)
         two_sb = load_list("two_sb", two)
         kidx_sb = load_list("kidx_sb", kidx)
         nc.sync.dma_start(ds_win[0:P:8, :].bitcast(I32), d_scales[0].bitcast(I32))
-        n1_sb = load_list("n1_sb", n1)
-        n2_sb = load_list("n2_sb", n2)
-        n3_sb = load_list("n3_sb", n3)
-        w2w_raw = sb("w2w_raw", [P, 2 * N], U8)
-        nc.sync.dma_start(w2w_raw[:].bitcast(I32), w2_words[0].bitcast(I32))
-        w3w_raw = sb("w3w_raw", [P, 2 * N], U8)
-        nc.sync.dma_start(w3w_raw[:].bitcast(I32), w3_words[0].bitcast(I32))
-        dw_win = sb("dw_win", [P, G], I32)
-        nc.sync.dma_start(dw_win[:], d_words[0].rearrange("p n t -> p (n t)").bitcast(I32))
-        w2s_raw = load_scale_rows("w2s_raw", w2_scales, on_sync)
-        w3s_raw = load_scale_rows("w3s_raw", w3_scales, on_sync)
-        gn_sb = sb("gn_sb", [P, PACK], F32)
-        nc.sync.dma_start(gn_sb[:], gn.rearrange("(p t) o -> p (t o)", t=PACK))
-        gk_sb = sb("gk_sb", [P, PACK], F32)
-        nc.sync.dma_start(gk_sb[:], gk.rearrange("(p t) o -> p (t o)", t=PACK))
+        y_lists = [load_list(f"n{i + 1}_sb", src) for i, src in enumerate((n1, n2, n3))]
+        w2w_raw = load_fp4_words("w2w_raw", w2_words)
+        w3w_raw = load_fp4_words("w3w_raw", w3_words)
+        dw_win = load_fp8_words("dw_win", d_words)
+        w2s_raw = load_scale_rows("w2s_raw", w2_scales)
+        w3s_raw = load_scale_rows("w3s_raw", w3_scales)
+        gn_sb = load_gain("gn_sb", gn)
+        gk_sb = load_gain("gk_sb", gk)
         n4_sb = load_list("n4_sb", n4)
         n5_sb = load_list("n5_sb", n5)
         n6_sb = load_list("n6_sb", n6)
 
-        y_win = [sb(f"y_win{t}", [P, 2 * S], F32) for t in range(PACK)]
-        sig_win = [sb(f"sig_win{t}", [P, S + SPARE], F32) for t in range(PACK)]
-        h_win = [sb(f"h_win{t}", [P, S + SPARE], F32) for t in range(PACK)]
+        y_win = [sb(f"y_win{t}", [P, 2 * S], F32) for t in range(PLANES)]
+        sig_win = [sb(f"sig_win{t}", [P, S + SPARE], F32) for t in range(PLANES)]
+        h_win = [sb(f"h_win{t}", [P, S + SPARE], F32) for t in range(PLANES)]
 
+        w1w = deal(nc.vector, sb("w1w", [P, 2 * H], U8)[:], w1w_raw[:], 2)
         xs_offs = sb("xs_offs", [P, S], U8)
-        gather(nc.vector, xs_offs[:], xs_win[:], offs_sb[:])
+        gather(True, xs_offs[:], xs_win[:], offs_sb[:])
         xw_offs = sb("xw_offs", [P, S], I32)
-        gather(nc.vector, xw_offs[:].bitcast(U32), xw_win[:].bitcast(U32), offs_sb[:])
-        w1w = deal(nc.gpsimd, sb("w1w", [P, 2 * H], U8)[:], w1w_raw[:], 2)
-        w1s = deal(nc.gpsimd, sb("w1s", [P, H], U8)[:], w1s_raw[:], 1)
-        y_ps = [psum.tile([P, S], F32, name=f"y_ps{t}", tag=f"bank{t}") for t in range(PACK)]
-        for t in range(PACK):
-            nc.tensor.matmul_mx(
-                out=y_ps[t][:],
-                lhsT=w1w[:, 256 * t : 256 * (t + 1)].bitcast(FP4X4),
-                lhsT_scale=w1s[:, P * t : P * (t + 1)],
-                rhs=xw_offs[:].bitcast(FP8X4),
-                rhs_scale=xs_offs[:],
-                start=True,
-                stop=True,
-            )
+        gather(True, xw_offs[:].bitcast(U32), xw_win[:].bitcast(U32), offs_sb[:])
+        w1s = deal(nc.vector, sb("w1s", [P, H], U8)[:], w1s_raw[:])
+        y_ps = [psum.tile([P, S], F32, name=f"y_ps{t}", tag=f"bank{t}") for t in range(PLANES)]
+        for t in (0, 2, 1, 3):
+            fp4_pass(y_ps[t][:], t, w1w, w1s, xw_offs[:], xs_offs[:], True, True)
 
         ds_kidx = sb("ds_kidx", [P, H], U8)
-        gather(nc.vector, ds_kidx[:], ds_win[:], kidx_sb[:])
-        ds_dealt = deal(nc.vector, sb("ds_dealt", [P, H], U8)[:], ds_kidx[:], 1)
+        gather(True, ds_kidx[:], ds_win[:], kidx_sb[:])
+        ds_dealt = deal(nc.vector, sb("ds_dealt", [P, H], U8)[:], ds_kidx[:])
         for q in range(4):
             nc.sync.dma_start(
                 ds_placed[32 * q : 32 * q + 4, :].bitcast(I32), ds_dealt[32 * q : 32 * q + 32 : 8, :].bitcast(I32)
             )
         xw_two = sb("xw_two", [P, S], I32)
-        gather(nc.vector, xw_two[:].bitcast(U32), xw_win[:].bitcast(U32), two_sb[:])
+        gather(True, xw_two[:].bitcast(U32), xw_win[:].bitcast(U32), two_sb[:])
         xs_two = sb("xs_two", [P, S], U8)
-        gather(nc.vector, xs_two[:], xs_win[:], two_sb[:])
+        gather(True, xs_two[:], xs_win[:], two_sb[:])
         dw_kidx = sb("dw_kidx", [P, H], I32)
-        gather(nc.vector, dw_kidx[:].bitcast(U32), dw_win[:].bitcast(U32), kidx_sb[:])
-        dw = deal(nc.vector, sb("dw", [P, H], I32)[:], dw_kidx[:], 1)
-        s_ps = [psum.tile([P, S], F32, name=f"s_ps{t}", tag=f"bank{PACK + t}") for t in range(PACK)]
-        for t in range(PACK):
+        gather(True, dw_kidx[:].bitcast(U32), dw_win[:].bitcast(U32), kidx_sb[:])
+        dw = deal(nc.vector, sb("dw", [P, H], I32)[:], dw_kidx[:])
+        s_ps = [psum.tile([P, S], F32, name=f"s_ps{t}", tag=f"bank{PLANES + t}") for t in range(PLANES)]
+        for t in range(PLANES):
             nc.tensor.matmul_mx(
                 out=s_ps[t][:],
                 lhsT=dw[:, P * t : P * (t + 1)].bitcast(FP8X4),
@@ -169,159 +178,146 @@ def tile_picked_jkeymixhopggpair_none_po_kernel(
 
         w23 = sb("w23", [P, 6 * N], U8, tag="dw_kidx")
         w2w = deal(nc.gpsimd, w23[:, 0 : 2 * N], w2w_raw[:], 2)
-        w2s = deal(nc.gpsimd, w23[:, 4 * N : 5 * N], w2s_raw[:], 1)
+        w2s = deal(nc.gpsimd, w23[:, 4 * N : 5 * N], w2s_raw[:])
         w3w = deal(nc.gpsimd, w23[:, 2 * N : 4 * N], w3w_raw[:], 2)
-        w3s = deal(nc.gpsimd, w23[:, 5 * N : 6 * N], w3s_raw[:], 1)
-        gk16 = sb("gk16", [P, PACK], F32)
+        w3s = deal(nc.gpsimd, w23[:, 5 * N : 6 * N], w3s_raw[:])
+        gk16 = sb("gk16", [P, PLANES], F32)
         nc.vector.tensor_scalar(gk16[:], gk_sb[:], 0.0625, None, ALU.mult)
 
-        on_vector = Y_AT_ON_VECTOR
-        after_d = sb("after_d", [P, 8 + len(on_vector), S], F32, tag="dw_win")
+        y_work = sb("y_work", [P, 2 * PLANES + len(Y_LOOKUPS_ON_VECTOR), S], F32, tag="dw_win")
         y_at = [
             [
-                after_d[:, 8 + on_vector.index((t, i)), :] if (t, i) in on_vector else sb(f"y_at{t}_{i}", [P, S], F32)[:]
+                y_work[:, 2 * PLANES + Y_LOOKUPS_ON_VECTOR.index((t, i)), :]
+                if (t, i) in Y_LOOKUPS_ON_VECTOR
+                else sb(f"y_at{t}_{i}", [P, S], F32)[:]
                 for i in range(3)
             ]
-            for t in range(PACK)
+            for t in range(PLANES)
         ]
-        top1 = [after_d[:, t, :] for t in range(PACK)]
-        top2 = [after_d[:, PACK + t, :] for t in range(PACK)]
-        gap = sb("gap", [P, PACK, S], F32)
-        y_lists = (n1_sb, n2_sb, n3_sb)
+        top1 = [y_work[:, t, :] for t in range(PLANES)]
+        top2 = [y_work[:, PLANES + t, :] for t in range(PLANES)]
+        gap = sb("gap", [P, PLANES, S], F32)
 
-        def y_out(t):
-            evacuate(nc.vector if t in Y_OUT_ON_VECTOR else nc.scalar, y_win[t][:, :S], y_ps[t][:])
+        def y_to_window(t):
+            nc.scalar.copy(y_win[t][:, :S], y_ps[t][:])
 
-        def y_gathers(t):
+        def y_lookups(t):
             for i in range(3):
-                engine = nc.vector if (t, i) in on_vector else nc.scalar
-                gather(engine, y_at[t][i], y_win[t][:], y_lists[i][:])
+                gather((t, i) in Y_LOOKUPS_ON_VECTOR, y_at[t][i], y_win[t][:], y_lists[i][:])
 
-        def y_tops(t):
+        def y_maxima(t):
             nc.vector.tensor_tensor(top1[t], y_at[t][0], y_ps[t][:], ALU.max)
             nc.vector.tensor_tensor(top2[t], y_at[t][1], y_at[t][2], ALU.max)
 
         def y_gap(t):
             nc.vector.tensor_tensor(gap[:, t, :], top1[t], top2[t], ALU.subtract)
 
-        y_out(0)
-        y_out(2)
-        y_gathers(2)
-        y_gathers(0)
-        y_tops(0)
-        y_out(1)
-        y_gathers(1)
-        y_tops(2)
+        y_to_window(0)
+        y_to_window(2)
+        y_lookups(2)
+        y_lookups(0)
+        y_maxima(0)
+        y_to_window(1)
+        y_lookups(1)
+        y_maxima(2)
         y_gap(0)
-        y_out(3)
-        y_gathers(3)
-        y_tops(1)
+        y_to_window(3)
+        y_lookups(3)
+        y_maxima(1)
         y_gap(2)
         y_gap(1)
-        y_tops(3)
+        y_maxima(3)
 
-        sig_at = [sb(f"sig_at{t}", [P, S], F32) for t in range(PACK)]
-        st = sb("st", [P, PACK, S], F32)
+        sig_at = [sb(f"sig_at{t}", [P, S], F32) for t in range(PLANES)]
+        st = sb("st", [P, PLANES, S], F32)
+        h_ends = [psum.tile([P, S - (LAST - MIDDLE)], F32, name=f"h_ends{t}", tag=f"bank{t}") for t in range(PLANES)]
+        z_bf = [sb(f"z_bf{u}", [P, HALF, PLANES], BF16) for u in range(2)]
+        z_w = [sb(f"z_w{u}", [P, HALF], I32) for u in range(2)]
+        z_s = [sb(f"z_s{u}", [P, HALF], U8) for u in range(2)]
 
         def s_gate(t):
             nc.scalar.activation(sig_win[t][:, :S], s_ps[t][:], ACT.Sigmoid, scale=0.0625)
-            gather(nc.scalar, sig_at[t][:], sig_win[t][:], n4_sb[:])
+            gather(False, sig_at[t][:], sig_win[t][:], n4_sb[:])
             nc.vector.scalar_tensor_tensor(
                 st[:, t, :], s_ps[t][:], gk16[:, t : t + 1], sig_at[t][:], ALU.mult, ALU.mult
             )
 
-        z_bf = sb("z_bf", [P, S, PACK], BF16)
-
-        def z_half(lo, hi):
+        def z_round(u):
             nc.vector.tensor_tensor(
-                weave_out(z_bf, lo, hi),
-                weave_in(gap, lo, hi),
-                gn_sb[:].unsqueeze(1).unsqueeze(3).to_broadcast([P, (hi - lo) // 4, PACK, 4]),
+                weave_out(z_bf[u][:]),
+                weave_in(gap[:, :, u * HALF : (u + 1) * HALF]),
+                gn_sb[:].unsqueeze(1).unsqueeze(3).to_broadcast([P, HALF // 4, PLANES, 4]),
                 ALU.mult,
             )
 
-        z_w = sb("z_w", [P, S], I32)
-        z_s = sb("z_s", [P, S], U8)
-        y_gap(3)
-        z_half(0, S // 2)
         s_gate(0)
-        z_half(S // 2, S)
+        y_gap(3)
         s_gate(1)
-        nc.vector.quantize_mx(out=z_w[:].bitcast(FP8X4), scales=z_s[:], in_=z_bf[:].rearrange("p j t -> p (j t)"))
+        z_round(0)
         s_gate(2)
+        quantize(z_w[0][:], z_s[0][:], z_bf[0][:])
         s_gate(3)
+        z_round(1)
+        quantize(z_w[1][:], z_s[1][:], z_bf[1][:])
 
-        h_ps = [psum.tile([P, S], F32, name=f"h_ps{t}", tag=f"bank{t}") for t in range(PACK)]
-        for t in range(PACK):
-            nc.tensor.matmul_mx(
-                out=h_ps[t][:],
-                lhsT=w2w[:, 256 * t : 256 * (t + 1)].bitcast(FP4X4),
-                lhsT_scale=w2s[:, P * t : P * (t + 1)],
-                rhs=z_w[:].bitcast(FP8X4),
-                rhs_scale=z_s[:],
-                start=True,
-                stop=False,
-            )
-
+        h_middle = [psum.tile([P, LAST - MIDDLE], F32, name=f"h_middle{t}", tag=f"bank{PLANES + t}") for t in range(PLANES)]
+        h_ps = {
+            FIRST: [h_ends[t][:, :MIDDLE] for t in range(PLANES)],
+            MIDDLE: [h_middle[t][:] for t in range(PLANES)],
+            LAST: [h_ends[t][:, MIDDLE:] for t in range(PLANES)],
+        }
         for lo, hi in CHUNKS:
             n = hi - lo
-            st_at = sb(f"st_at{lo}", [P, PACK, n], F32)
-            z2_bf = sb(f"z2_bf{lo}", [P, n, PACK], BF16)
+            u, cols = lo // HALF, slice(lo % HALF, lo % HALF + n)
+            for t in range(PLANES):
+                fp4_pass(h_ps[lo][t], t, w2w, w2s, z_w[u][:, cols], z_s[u][:, cols], True, False)
+            st_at = sb(f"st_at{lo}", [P, PLANES, n], F32)
+            z2_bf = sb(f"z2_bf{lo}", [P, n, PLANES], BF16, tag="z_bf1")
             z2_w = sb(f"z2_w{lo}", [P, n], I32)
             z2_s = sb(f"z2_s{lo}", [P, n], U8)
-            for t in range(PACK):
-                window = st[:, t, :] if lo == 0 else st[:, t:, :].rearrange("p t j -> p (t j)")
-                gather(nc.scalar, st_at[:, t, :], window, n5_sb[:, lo // 16 : hi // 16])
-            nc.vector.tensor_tensor(weave_out(z2_bf, 0, n), weave_in(st, lo, hi), weave_in(st_at, 0, n), ALU.subtract)
-            nc.vector.quantize_mx(out=z2_w[:].bitcast(FP8X4), scales=z2_s[:], in_=z2_bf[:].rearrange("p j t -> p (j t)"))
-            for t in range(PACK):
-                nc.tensor.matmul_mx(
-                    out=h_ps[t][:, lo:hi],
-                    lhsT=w3w[:, 256 * t : 256 * (t + 1)].bitcast(FP4X4),
-                    lhsT_scale=w3s[:, P * t : P * (t + 1)],
-                    rhs=z2_w[:].bitcast(FP8X4),
-                    rhs_scale=z2_s[:],
-                    start=False,
-                    stop=(hi == S),
-                )
+            for t in range(PLANES):
+                window = st[:, t, :] if lo == FIRST else st[:, t:, :].rearrange("p t j -> p (t j)")
+                gather(False, st_at[:, t, :], window, n5_sb[:, lo // 16 : hi // 16])
+            nc.vector.tensor_tensor(weave_out(z2_bf[:]), weave_in(st[:, :, lo:hi]), weave_in(st_at[:]), ALU.subtract)
+            quantize(z2_w[:], z2_s[:], z2_bf[:])
+            for t in range(PLANES):
+                fp4_pass(h_ps[lo][t], t, w3w, w3s, z2_w[:], z2_s[:], False, True)
+            for t in range(PLANES):
+                plain_copy(lo == LAST and t % 2 == 1, h_win[t][:, lo:hi], h_ps[lo][t])
 
-        for t in range(PACK):
-            evacuate(nc.scalar if t in H_ON_SCALAR else nc.vector, h_win[t][:, :S], h_ps[t][:])
         res_w = sb("res_w", [P, S], I32)
         res_s = sb("res_s", [P, S], U8)
-        out_rows = out_0.rearrange("(p t) j -> p t j", t=PACK)
+        out_rows = out_0.rearrange("(p t) j -> p t j", t=PLANES)
         out_words = out_1[0].rearrange("p n t -> p (n t)").bitcast(I32)
-        all_members = {}
-        for lo, hi in OUT_CHUNKS:
-            members = [sb(f"members{lo}_{u}", [P, 2, hi - lo, 2], F32) for u in range(2)]
-            all_members[lo] = members
-            for t in range(PACK):
+        members = {}
+        for lo, hi in CHUNKS:
+            members[lo] = [sb(f"members{lo}_{pair}", [P, 2, hi - lo, 2], F32) for pair in range(2)]
+            for t in range(PLANES):
                 gather(
-                    nc.vector if (lo, t) in OUT_ON_VECTOR else nc.scalar,
-                    members[t // 2][:, t % 2, :, :].rearrange("p j e -> p (j e)"),
+                    (lo, t) in H_LOOKUPS_ON_VECTOR,
+                    members[lo][t // 2][:, t % 2, :, :].rearrange("p j e -> p (j e)"),
                     h_win[t][:],
-                    n6_sb[:, lo // 8 : hi // 8],
+                    n6_sb[:, 2 * lo // 16 : 2 * hi // 16],
                 )
-        for lo, hi in OUT_CHUNKS:
+        for lo, hi in CHUNKS:
             n = hi - lo
-            members = all_members[lo]
-            under = sb(f"under{lo}", [P, PACK, n], F32)
-            left = sb(f"left{lo}", [P, PACK, n], F32)
-            res = sb(f"res{lo}", [P, PACK, n], F32)
-            res_bf = sb(f"res_bf{lo}", [P, n, PACK], BF16)
-            for t in range(PACK):
-                nc.vector.tensor_tensor(under[:, t, :], members[t // 2][:, t % 2, :, 1], h_ps[t][:, lo:hi], ALU.subtract)
-            for u in range(2):
-                pair = slice(2 * u, 2 * u + 2)
-                nc.vector.scalar_tensor_tensor(left[:, pair, :], under[:, pair, :], 0.0, members[u][:, :, :, 0], ALU.min, ALU.add)
-            for u in range(2):
-                pair = slice(2 * u, 2 * u + 2)
-                nc.vector.tensor_tensor(res[:, pair, :], left[:, pair, :], members[u][:, :, :, 1], ALU.min)
+            b_less_h = sb(f"b_less_h{lo}", [P, PLANES, n], F32)
+            a_part = sb(f"a_part{lo}", [P, PLANES, n], F32)
+            res = sb(f"res{lo}", [P, PLANES, n], F32)
+            res_bf = sb(f"res_bf{lo}", [P, n, PLANES], BF16)
+            for t in range(PLANES):
+                nc.vector.tensor_tensor(b_less_h[:, t, :], members[lo][t // 2][:, t % 2, :, 1], h_ps[lo][t], ALU.subtract)
+            for pair in range(2):
+                both = slice(2 * pair, 2 * pair + 2)
+                nc.vector.scalar_tensor_tensor(
+                    a_part[:, both, :], b_less_h[:, both, :], 0.0, members[lo][pair][:, :, :, 0], ALU.min, ALU.add
+                )
+            for pair in range(2):
+                both = slice(2 * pair, 2 * pair + 2)
+                nc.vector.tensor_tensor(res[:, both, :], a_part[:, both, :], members[lo][pair][:, :, :, 1], ALU.min)
             nc.sync.dma_start(out_rows[:, :, lo:hi], res[:])
-            evacuate(nc.scalar if lo in ROUND_ON_SCALAR else nc.vector, weave_out(res_bf, 0, n), weave_in(res, 0, n))
-            nc.vector.quantize_mx(
-                out=res_w[:, lo:hi].bitcast(FP8X4), scales=res_s[:, lo:hi], in_=res_bf[:].rearrange("p j t -> p (j t)")
-            )
+            plain_copy(lo != MIDDLE, weave_out(res_bf[:]), weave_in(res[:]))
+            quantize(res_w[:, lo:hi], res_s[:, lo:hi], res_bf[:])
             nc.sync.dma_start(out_words[:, lo:hi], res_w[:, lo:hi])
         for q in range(4):
             queue = nc.scalar if q % 2 else nc.sync

from contextlib import ExitStack

import concourse.mybir as mybir

S, N, H, G = 512, 512, 512, 2048
FLOPS = 4 * 2 * 512 * 512 * 512

F32 = mybir.dt.float32
BF16 = mybir.dt.bfloat16
I32 = mybir.dt.int32
U32 = mybir.dt.uint32
U16 = mybir.dt.uint16
U8 = mybir.dt.uint8
FP8X4 = mybir.dt.float8_e4m3fn_x4
FP4X4 = mybir.dt.float4_e2m1fn_x4
ALU = mybir.AluOpType
ACT = mybir.ActivationFunctionType

P = 128
PLANES = 4
HALF = S // 2
FIRST, MIDDLE, LAST = 0, 256, 384
CHUNKS = ((FIRST, MIDDLE), (MIDDLE, LAST), (LAST, S))
SPARE = 16
Y_LOOKUPS_ON_VECTOR = ((2, 0), (2, 1), (2, 2), (3, 0))
H_LOOKUPS_ON_VECTOR = ((FIRST, 1), (MIDDLE, 1))


def tile_picked_jkeymixhopggpair_none_po_kernel(
    tc, x_words, x_scales, w1_words, w1_scales, d_words, d_scales, gn, gk, w2_words, w2_scales, w3_words, w3_scales,
    offs, kidx, two, n1, n2, n3, n4, n5, n6, out_0, out_1, out_2,
):
    nc = tc.nc
    with ExitStack() as ctx:
        keep = ctx.enter_context(tc.tile_pool(name="keep", bufs=1))
        psum = ctx.enter_context(tc.psum_pool(name="psum", bufs=1))

        def sb(name, shape, dtype, tag=None):
            return keep.tile(shape, dtype, name=name, tag=tag or name, align_bytes=64)

        def load_list(name, src):
            tile = keep.tile(list(src.shape), U16, name=name)
            nc.sync.dma_start(tile[:], src)
            return tile

        def load_fp8_words(name, src):
            tile = sb(name, [P, src.shape[2]], I32)
            nc.sync.dma_start(tile[:], src[0].rearrange("p n t -> p (n t)").bitcast(I32))
            return tile

        def load_fp4_words(name, src):
            tile = sb(name, [P, src.shape[2]], U8)
            nc.sync.dma_start(tile[:].bitcast(I32), src[0].bitcast(I32))
            return tile

        def load_scale_rows(name, src):
            width = src.shape[2]
            tile = sb(name, [P, width], U8)
            for q in range(4):
                rows = src[:, 4 * q : 4 * q + 4, :].bitcast(I32)
                nc.sync.dma_start(tile[32 * q : 32 * q + 32, :].bitcast(I32), rows.to_broadcast([8, 4, width // 4]))
            return tile

        def load_gain(name, src):
            tile = sb(name, [P, PLANES], F32)
            nc.sync.dma_start(tile[:], src.rearrange("(p t) o -> p (t o)", t=PLANES))
            return tile

        def zeroed_bytes(name, width):
            tile = sb(name, [P, width], U8)
            nc.vector.memset(tile[:].bitcast(I32), 0)
            return tile

        def deal(engine, dealt, src, per_column=1):
            engine.tensor_copy(
                dealt.rearrange("p (t m b) -> p t m b", t=PLANES, b=per_column),
                src.rearrange("p (m t b) -> p t m b", t=PLANES, b=per_column),
            )
            return dealt

        def gather(on_vector, out, window, offsets):
            if on_vector:
                nc.vector.tensor_copy(out, window.indirect(offsets))
            else:
                nc.scalar.activation(out, window.indirect(offsets), ACT.Copy)

        def plain_copy(on_vector, out, src):
            if on_vector:
                nc.vector.tensor_copy(out, src)
            else:
                nc.scalar.copy(out, src)

        def weave_in(planes):
            return planes.rearrange("p t (c i) -> p c t i", i=4)

        def weave_out(woven):
            return woven.rearrange("p (c i) t -> p c t i", i=4)

        def quantize(words, scales, woven):
            nc.vector.quantize_mx(out=words.bitcast(FP8X4), scales=scales, in_=woven.rearrange("p j t -> p (j t)"))

        def fp4_pass(out, t, w_words, w_scales, words, scales, start, stop):
            nc.tensor.matmul_mx(
                out=out,
                lhsT=w_words[:, 2 * P * t : 2 * P * (t + 1)].bitcast(FP4X4),
                lhsT_scale=w_scales[:, P * t : P * (t + 1)],
                rhs=words.bitcast(FP8X4),
                rhs_scale=scales,
                start=start,
                stop=stop,
            )

        warm = sb("warm", [P, 2], F32)
        nc.vector.memset(warm[:, 0:1], 0.0)
        nc.scalar.activation(warm[:, 1:2], warm[:, 0:1], ACT.Sigmoid)

        ds_win = zeroed_bytes("ds_win", G)
        ds_placed = zeroed_bytes("ds_placed", H)
        w1w_raw = load_fp4_words("w1w_raw", w1_words)
        offs_sb = load_list("offs_sb", offs)
        xs_win = load_scale_rows("xs_win", x_scales)
        xw_win = load_fp8_words("xw_win", x_words)
        w1s_raw = load_scale_rows("w1s_raw", w1_scales)
        two_sb = load_list("two_sb", two)
        kidx_sb = load_list("kidx_sb", kidx)
        nc.sync.dma_start(ds_win[0:P:8, :].bitcast(I32), d_scales[0].bitcast(I32))
        y_lists = [load_list(f"n{i + 1}_sb", src) for i, src in enumerate((n1, n2, n3))]
        w2w_raw = load_fp4_words("w2w_raw", w2_words)
        w3w_raw = load_fp4_words("w3w_raw", w3_words)
        dw_win = load_fp8_words("dw_win", d_words)
        w2s_raw = load_scale_rows("w2s_raw", w2_scales)
        w3s_raw = load_scale_rows("w3s_raw", w3_scales)
        gn_sb = load_gain("gn_sb", gn)
        gk_sb = load_gain("gk_sb", gk)
        n4_sb = load_list("n4_sb", n4)
        n5_sb = load_list("n5_sb", n5)
        n6_sb = load_list("n6_sb", n6)

        y_win = [sb(f"y_win{t}", [P, 2 * S], F32) for t in range(PLANES)]
        sig_win = [sb(f"sig_win{t}", [P, S + SPARE], F32) for t in range(PLANES)]
        h_win = [sb(f"h_win{t}", [P, S + SPARE], F32) for t in range(PLANES)]

        w1w = deal(nc.vector, sb("w1w", [P, 2 * H], U8)[:], w1w_raw[:], 2)
        xs_offs = sb("xs_offs", [P, S], U8)
        gather(True, xs_offs[:], xs_win[:], offs_sb[:])
        xw_offs = sb("xw_offs", [P, S], I32)
        gather(True, xw_offs[:].bitcast(U32), xw_win[:].bitcast(U32), offs_sb[:])
        w1s = deal(nc.vector, sb("w1s", [P, H], U8)[:], w1s_raw[:])
        y_ps = [psum.tile([P, S], F32, name=f"y_ps{t}", tag=f"bank{t}") for t in range(PLANES)]
        for t in (0, 2, 1, 3):
            fp4_pass(y_ps[t][:], t, w1w, w1s, xw_offs[:], xs_offs[:], True, True)

        ds_kidx = sb("ds_kidx", [P, H], U8)
        gather(True, ds_kidx[:], ds_win[:], kidx_sb[:])
        ds_dealt = deal(nc.vector, sb("ds_dealt", [P, H], U8)[:], ds_kidx[:])
        for q in range(4):
            nc.sync.dma_start(
                ds_placed[32 * q : 32 * q + 4, :].bitcast(I32), ds_dealt[32 * q : 32 * q + 32 : 8, :].bitcast(I32)
            )
        xw_two = sb("xw_two", [P, S], I32)
        gather(True, xw_two[:].bitcast(U32), xw_win[:].bitcast(U32), two_sb[:])
        xs_two = sb("xs_two", [P, S], U8)
        gather(True, xs_two[:], xs_win[:], two_sb[:])
        dw_kidx = sb("dw_kidx", [P, H], I32)
        gather(True, dw_kidx[:].bitcast(U32), dw_win[:].bitcast(U32), kidx_sb[:])
        dw = deal(nc.vector, sb("dw", [P, H], I32)[:], dw_kidx[:])
        s_ps = [psum.tile([P, S], F32, name=f"s_ps{t}", tag=f"bank{PLANES + t}") for t in range(PLANES)]
        for t in range(PLANES):
            nc.tensor.matmul_mx(
                out=s_ps[t][:],
                lhsT=dw[:, P * t : P * (t + 1)].bitcast(FP8X4),
                lhsT_scale=ds_placed[:, P * t : P * (t + 1)],
                rhs=xw_two[:].bitcast(FP8X4),
                rhs_scale=xs_two[:],
                start=True,
                stop=True,
            )

        w23 = sb("w23", [P, 6 * N], U8, tag="dw_kidx")
        w2w = deal(nc.gpsimd, w23[:, 0 : 2 * N], w2w_raw[:], 2)
        w2s = deal(nc.gpsimd, w23[:, 4 * N : 5 * N], w2s_raw[:])
        w3w = deal(nc.gpsimd, w23[:, 2 * N : 4 * N], w3w_raw[:], 2)
        w3s = deal(nc.gpsimd, w23[:, 5 * N : 6 * N], w3s_raw[:])
        gk16 = sb("gk16", [P, PLANES], F32)
        nc.vector.tensor_scalar(gk16[:], gk_sb[:], 0.0625, None, ALU.mult)

        y_work = sb("y_work", [P, 2 * PLANES + len(Y_LOOKUPS_ON_VECTOR), S], F32, tag="dw_win")
        y_at = [
            [
                y_work[:, 2 * PLANES + Y_LOOKUPS_ON_VECTOR.index((t, i)), :]
                if (t, i) in Y_LOOKUPS_ON_VECTOR
                else sb(f"y_at{t}_{i}", [P, S], F32)[:]
                for i in range(3)
            ]
            for t in range(PLANES)
        ]
        top1 = [y_work[:, t, :] for t in range(PLANES)]
        top2 = [y_work[:, PLANES + t, :] for t in range(PLANES)]
        gap = sb("gap", [P, PLANES, S], F32)

        def y_to_window(t):
            nc.scalar.copy(y_win[t][:, :S], y_ps[t][:])

        def y_lookups(t):
            for i in range(3):
                gather((t, i) in Y_LOOKUPS_ON_VECTOR, y_at[t][i], y_win[t][:], y_lists[i][:])

        def y_maxima(t):
            nc.vector.tensor_tensor(top1[t], y_at[t][0], y_ps[t][:], ALU.max)
            nc.vector.tensor_tensor(top2[t], y_at[t][1], y_at[t][2], ALU.max)

        def y_gap(t):
            nc.vector.tensor_tensor(gap[:, t, :], top1[t], top2[t], ALU.subtract)

        y_to_window(0)
        y_to_window(2)
        y_lookups(2)
        y_lookups(0)
        y_maxima(0)
        y_to_window(1)
        y_lookups(1)
        y_maxima(2)
        y_gap(0)
        y_to_window(3)
        y_lookups(3)
        y_maxima(1)
        y_gap(2)
        y_gap(1)
        y_maxima(3)

        sig_at = [sb(f"sig_at{t}", [P, S], F32) for t in range(PLANES)]
        st = sb("st", [P, PLANES, S], F32)
        h_ends = [psum.tile([P, S - (LAST - MIDDLE)], F32, name=f"h_ends{t}", tag=f"bank{t}") for t in range(PLANES)]
        z_bf = [sb(f"z_bf{u}", [P, HALF, PLANES], BF16) for u in range(2)]
        z_w = [sb(f"z_w{u}", [P, HALF], I32) for u in range(2)]
        z_s = [sb(f"z_s{u}", [P, HALF], U8) for u in range(2)]

        def s_gate(t):
            nc.scalar.activation(sig_win[t][:, :S], s_ps[t][:], ACT.Sigmoid, scale=0.0625)
            gather(False, sig_at[t][:], sig_win[t][:], n4_sb[:])
            nc.vector.scalar_tensor_tensor(
                st[:, t, :], s_ps[t][:], gk16[:, t : t + 1], sig_at[t][:], ALU.mult, ALU.mult
            )

        def z_round(u):
            nc.vector.tensor_tensor(
                weave_out(z_bf[u][:]),
                weave_in(gap[:, :, u * HALF : (u + 1) * HALF]),
                gn_sb[:].unsqueeze(1).unsqueeze(3).to_broadcast([P, HALF // 4, PLANES, 4]),
                ALU.mult,
            )

        s_gate(0)
        y_gap(3)
        s_gate(1)
        z_round(0)
        s_gate(2)
        quantize(z_w[0][:], z_s[0][:], z_bf[0][:])
        s_gate(3)
        z_round(1)
        quantize(z_w[1][:], z_s[1][:], z_bf[1][:])

        h_middle = [psum.tile([P, LAST - MIDDLE], F32, name=f"h_middle{t}", tag=f"bank{PLANES + t}") for t in range(PLANES)]
        h_ps = {
            FIRST: [h_ends[t][:, :MIDDLE] for t in range(PLANES)],
            MIDDLE: [h_middle[t][:] for t in range(PLANES)],
            LAST: [h_ends[t][:, MIDDLE:] for t in range(PLANES)],
        }
        for lo, hi in CHUNKS:
            n = hi - lo
            u, cols = lo // HALF, slice(lo % HALF, lo % HALF + n)
            for t in range(PLANES):
                fp4_pass(h_ps[lo][t], t, w2w, w2s, z_w[u][:, cols], z_s[u][:, cols], True, False)
            st_at = sb(f"st_at{lo}", [P, PLANES, n], F32)
            z2_bf = sb(f"z2_bf{lo}", [P, n, PLANES], BF16, tag="z_bf1")
            z2_w = sb(f"z2_w{lo}", [P, n], I32)
            z2_s = sb(f"z2_s{lo}", [P, n], U8)
            for t in range(PLANES):
                window = st[:, t, :] if lo == FIRST else st[:, t:, :].rearrange("p t j -> p (t j)")
                gather(False, st_at[:, t, :], window, n5_sb[:, lo // 16 : hi // 16])
            nc.vector.tensor_tensor(weave_out(z2_bf[:]), weave_in(st[:, :, lo:hi]), weave_in(st_at[:]), ALU.subtract)
            quantize(z2_w[:], z2_s[:], z2_bf[:])
            for t in range(PLANES):
                fp4_pass(h_ps[lo][t], t, w3w, w3s, z2_w[:], z2_s[:], False, True)
            for t in range(PLANES):
                plain_copy(lo == LAST and t % 2 == 1, h_win[t][:, lo:hi], h_ps[lo][t])

        res_w = sb("res_w", [P, S], I32)
        res_s = sb("res_s", [P, S], U8)
        out_rows = out_0.rearrange("(p t) j -> p t j", t=PLANES)
        out_words = out_1[0].rearrange("p n t -> p (n t)").bitcast(I32)
        members = {}
        for lo, hi in CHUNKS:
            members[lo] = [sb(f"members{lo}_{pair}", [P, 2, hi - lo, 2], F32) for pair in range(2)]
            for t in range(PLANES):
                gather(
                    (lo, t) in H_LOOKUPS_ON_VECTOR,
                    members[lo][t // 2][:, t % 2, :, :].rearrange("p j e -> p (j e)"),
                    h_win[t][:],
                    n6_sb[:, 2 * lo // 16 : 2 * hi // 16],
                )
        for lo, hi in CHUNKS:
            n = hi - lo
            b_less_h = sb(f"b_less_h{lo}", [P, PLANES, n], F32)
            a_part = sb(f"a_part{lo}", [P, PLANES, n], F32)
            res = sb(f"res{lo}", [P, PLANES, n], F32)
            res_bf = sb(f"res_bf{lo}", [P, n, PLANES], BF16)
            for t in range(PLANES):
                nc.vector.tensor_tensor(b_less_h[:, t, :], members[lo][t // 2][:, t % 2, :, 1], h_ps[lo][t], ALU.subtract)
            for pair in range(2):
                both = slice(2 * pair, 2 * pair + 2)
                nc.vector.scalar_tensor_tensor(
                    a_part[:, both, :], b_less_h[:, both, :], 0.0, members[lo][pair][:, :, :, 0], ALU.min, ALU.add
                )
            for pair in range(2):
                both = slice(2 * pair, 2 * pair + 2)
                nc.vector.tensor_tensor(res[:, both, :], a_part[:, both, :], members[lo][pair][:, :, :, 1], ALU.min)
            nc.sync.dma_start(out_rows[:, :, lo:hi], res[:])
            plain_copy(lo != MIDDLE, weave_out(res_bf[:]), weave_in(res[:]))
            quantize(res_w[:, lo:hi], res_s[:, lo:hi], res_bf[:])
            nc.sync.dma_start(out_words[:, lo:hi], res_w[:, lo:hi])
        for q in range(4):
            queue = nc.scalar if q % 2 else nc.sync
            queue.dma_start(out_2[0, 4 * q : 4 * q + 4, :].bitcast(I32), res_s[32 * q : 32 * q + 4, :].bitcast(I32))
